import numpy as np
CORES = [56,61,80,85]
N = 4
T, FF, CAPT = 2048, 32, 2048
def entries(a): return a.T.reshape(-1)
def pack(v, P): return np.ascontiguousarray(np.asarray(v, np.int32).reshape(-1, P).T)
def lists(rng, how):
    w = rng.random(N) ** 2 + 1e-3; c = T // 8 + ((CAPT - N * (T // 8)) * w / w.sum()).astype(np.int64)
    a = rng.permutation(N)
    if how == "few": c = np.zeros(N, np.int64); c[N - 1] = 3; c[int(rng.integers(N - 1))] = 1
    if how == "lone": s = int(rng.integers(CAPT - T + 1)); c = np.zeros(N, np.int64); c[a[0]] = T; c[a[1]] = s; c[a[2]] = CAPT - T - s
    if how == "none": c = np.zeros(N, np.int64)
    if how == "pair": s = 2 * int(rng.integers(512, 767)) + 1; c = np.zeros(N, np.int64); c[a[0]] = s; c[a[1]] = CAPT - s - 1; c[a[2]] = 1
    if how == "zeros": c = np.full(N, 2); c[0] = T - 7 - 2 * int(rng.integers(T // 16))
    K = np.stack([rng.permutation(np.arange(T) < c[r]) for r in range(N)])
    if how == "zeros": K = np.stack([np.r_[True, rng.permutation(np.arange(T - 2) < c[r] - 2), True] for r in range(N)])
    return {"keep": np.stack([pack(k, 16) for k in K])}
def blank(d):
    for r in range(N):
        k = entries(d["keep"][r]); d["x"][r][:, np.nonzero(k)[0][1:-1:4]] = 0; d["x"][r][:, np.nonzero(1 - k)[0][::4]] = 0
def setup_inputs(rng):
    return dict({"x": rng.standard_normal((N, 128, T), dtype=np.float32), "w1": np.repeat((rng.standard_normal((1, 128, FF * 128), dtype=np.float32) / 8), N, axis=0), "w2": np.repeat((rng.standard_normal((1, 128, FF * 128), dtype=np.float32) / 64), N, axis=0)}, **lists(rng, "uniform"))
def setup_inputs_few(rng):
    d = setup_inputs(rng); d.update(lists(rng, "few"))
    for k in ("x",): d[k] = (d[k].astype(np.float32) * 1024.0).astype(d[k].dtype)
    return d
def setup_inputs_lone(rng):
    d = setup_inputs(rng); d.update(lists(rng, "lone"))
    for k in ("x",): d[k] = (d[k].astype(np.float32) * (1 / 1024.0)).astype(d[k].dtype)
    return d
def setup_inputs_none(rng):
    d = setup_inputs(rng); d.update(lists(rng, "none"))
    return d
def setup_inputs_pair(rng):
    d = setup_inputs(rng); d.update(lists(rng, "pair"))
    return d
def setup_inputs_zeros(rng):
    d = setup_inputs(rng); d.update(lists(rng, "zeros"))
    blank(d)
    return d
def check_inputs(x):
    bad = []
    if x["keep"].min() < 0 or x["keep"].max() >= 2: bad.append("keep out of range")
    if int(x["keep"].sum()) > CAPT: bad.append("more than CAPT tokens are kept in all")
    if any((x[k] != x[k][:1]).any() for k in ("w1", "w2")): bad.append("w1 or w2 is not alike on all ranks")
    return bad
def reference(x, w1, w2, keep):
    X, W1, W2 = x.astype(np.float64), w1.astype(np.float64), w2.astype(np.float64)
    Y = X.copy()
    for r in range(N):
        P = np.nonzero(entries(keep[r]) == 1)[0]
        if len(P) == 0: continue
        Y[r][:, P] = sum(W2[r][:, 128 * f:128 * f + 128].T @ np.maximum(W1[r][:, 128 * f:128 * f + 128].T @ X[r][:, P], 0.0) for f in range(FF))
    return {"y": Y.astype(np.float32)}

@@ -1,0 +1,447 @@
+import numpy as np
+from concourse.bass import DstId, RemoteDMATransfer
+from concourse.mybir import dt, AluOpType as Op, AxisListType, ActivationFunctionType as Act
+
+NH = 2
+NS = 72
+NCORES = 96
+NU = 16
+UW = 512
+RB = 2052
+NB = 6
+WMAX = 8192
+
+INTS = ("pid", "ri", "g2i", "q7i", "q3i")
+COLS = ("m0", "m1", "m2", "m23", "w3", "g2f", "q7f", "q3f", "w01", "w2c", "wa", "wc", "tcol")
+SCRATCH = {
+    "cint": ("sbuf", [128, 8], "int32"),
+    "cflt": ("sbuf", [128, 16], "float32"),
+    "xw": ("sbuf", [128, RB + 2048], "float32"),
+    "wb": ("sbuf", [128, NU * UW], "float32"),
+    "xg": ("sbuf", [128, 2048], "float32"),
+    "ta": ("sbuf", [128, 256], "float32"),
+    "tb": ("sbuf", [128, 256], "float32"),
+    "xm": ("sbuf", [128, 256], "float32"),
+    "hb": ("sbuf", [128, NU * 256], "float32"),
+    "yo": ("sbuf", [128, 256], "float32"),
+    "yb": ("sbuf", [128, 2048], "float32"),
+    "win": ("sbuf", [128, WMAX], "bfloat16"),
+    "vals": ("sbuf", [128, 256], "bfloat16"),
+    "zsel": ("sbuf", [128, 144], "bfloat16"),
+    "fa": ("sbuf", [128, 256], "float32"),
+    "fb": ("sbuf", [128, 256], "float32"),
+    "fc": ("sbuf", [128, 256], "float32"),
+    "fd": ("sbuf", [128, 256], "float32"),
+    "fsel": ("sbuf", [128, 144], "float32"),
+    "fdiff": ("sbuf", [128, 128], "float32"),
+    "tri": ("sbuf", [128, 128], "float32"),
+    "ki": ("sbuf", [128, 16], "int32"),
+    "kf": ("sbuf", [128, 16], "float32"),
+    "ones": ("sbuf", [128, 16], "float32"),
+    "scn": ("sbuf", [128, 16], "float32"),
+    "dump": ("sbuf", [128, 16], "float32"),
+    "c16": ("sbuf", [128, 16], "float32"),
+    "cz": ("sbuf", [128, 16], "float32"),
+    "pa": ("sbuf", [128, 16], "float32"),
+    "pb": ("sbuf", [128, 16], "float32"),
+    "pp": ("sbuf", [128, 16], "float32"),
+    "tq": ("sbuf", [128, 16], "float32"),
+    "tqm": ("sbuf", [128, 16], "float32"),
+    "ga": ("sbuf", [128, 16], "float32"),
+    "gb": ("sbuf", [128, 16], "float32"),
+    "gd": ("sbuf", [128, 16], "float32"),
+    "ge": ("sbuf", [128, 16], "float32"),
+    "offs": ("sbuf", [128, 16], "uint16"),
+    "ysrc": ("sbuf", [128, 16], "uint16"),
+    "listx": ("sbuf", [128, 64], "uint16"),
+    "listy": ("sbuf", [128, 64], "uint16"),
+    "ylist": ("sbuf", [128, 128], "uint16"),
+    "ydram": ("dram", [128, 16], "uint16"),
+    "yacc": ("psum", [128, 512], "float32"),
+}
+for _n in range(NB):
+    SCRATCH["h%d" % _n] = ("psum", [128, 512], "float32")
+
+SEMAPHORES = ["io1", "io2", "vs", "sg", "tm", "tx", "ty", "kd", "xd", "tka", "tkb", "tkh", "mg1", "mg2", "yd", "yc",
+              "res", "loc", "yl1", "yl2", "fv", "fs", "ys", "yt"]
+SEMAPHORES += ["w%d" % u for u in range(NU)] + ["ld%d" % u for u in range(NU)]
+SEMAPHORES += ["l%d" % u for u in range(NU)] + ["r%d" % u for u in range(NU)]
+
+
+def _count(mask):
+    return bin(mask).count("1")
+
+
+def _split(mask, k):
+    eng = [e for e in range(mask.bit_length()) if mask >> e & 1]
+    per = 1
+    while per * 2 * k <= len(eng):
+        per *= 2
+    return [sum(1 << e for e in eng[i * per:(i + 1) * per]) for i in range(k)]
+
+
+def _teams(T, topo):
+    homes = []
+    for c in T.cores:
+        if topo.chip(c) not in homes:
+            homes.append(topo.chip(c))
+    chips = []
+    for c in range(NCORES):
+        if topo.chip(c) not in chips:
+            chips.append(topo.chip(c))
+    teams, used = [], list(homes)
+    for h in homes:
+        ranks = [c for c in T.cores if topo.chip(c) == h]
+        dies = [topo.die(c) for c in ranks]
+
+        def halves(chip):
+            out = []
+            for s in range(2):
+                cs = [c for c in range(NCORES) if topo.chip(c) == chip and topo.die(c) == dies[s]]
+                out.append([c for c in cs if c in ranks] + [c for c in cs if c not in ranks])
+            return out
+        free = [c for c in chips if c not in used and topo.same_plane(h, c)]
+        far = [c for c in free if not any(topo.mates(c, x) for x in homes)]
+        helpers = (far + [c for c in free if c not in far])[:NH]
+        used += helpers
+        teams.append({"ranks": ranks, "chips": [halves(h)] + [halves(c) for c in helpers]})
+    return teams
+
+
+def _route(u):
+    return [1 + (u + i) % NH for i in range(NH)]
+
+
+def _pos(u, ci):
+    return 0 if ci == 0 else 1 + _route(u).index(ci)
+
+
+def _order(ci):
+    def key(u):
+        ul = u % 8
+        return (ul // 2 * 2 + (3 if ul >= 4 else 0) + 4 * _pos(u, ci), ul, u)
+    return sorted(range(NU), key=key)
+
+
+def _owner(team, u, ci):
+    s, ul = u // 8, u % 8
+    return team["chips"][ci][s][1 + ul % 3] if ci == 0 else team["chips"][ci][s][ul % 4]
+
+
+def rank_program(g, core, T, topo):
+    team = None
+    for t in _teams(T, topo):
+        for ci, hv in enumerate(t["chips"]):
+            if core in hv[0] + hv[1]:
+                team, chip_i = t, ci
+    if team is None:
+        return
+    ranks = team["ranks"]
+    home = team["chips"][0][0] + team["chips"][0][1]
+    mine = team["chips"][chip_i][0] + team["chips"][chip_i][1]
+    wi = mine.index(core)
+    side = ranks.index(core) if core in ranks else None
+    n = 256 - NH * NS if chip_i == 0 else NS
+    first = NH * NS if chip_i == 0 else (chip_i - 1) * NS
+    S = T.sem
+    on = topo.mask(core, [c for c in mine if c != core][0])
+    loc = [0]
+
+    def I(name):
+        k = INTS.index(name)
+        return T.cint[:, k:k + 1]
+
+    def C(name):
+        k = COLS.index(name)
+        return T.cflt[:, k:k + 1]
+
+    def did(c):
+        rid, pid, _ = topo.addr(c)
+        return DstId(rid=rid, pnc=pid)
+
+    def send(parts):
+        g.remote_dma_fused([RemoteDMATransfer(dst_ids=[did(c) for c in ds], dma_engine_mask=m, remote_sem=sem,
+                                              srcs=[src], dsts=[dst] * len(ds)) for src, dst, ds, m, sem in parts],
+                           local_sem=S.loc)
+        loc[0] += sum(_count(p[3]) for p in parts)
+
+    def unit(u):
+        return T.wb[:, UW * u:UW * (u + 1)]
+
+    def arrival(u):
+        own = _owner(team, u, chip_i)
+        if core != own:
+            return _count(on)
+        if chip_i == 0:
+            return _count(_split(on, 2)[0])
+        r = _route(u)
+        p = r.index(chip_i)
+        src = _owner(team, u, r[p - 1] if p else 0)
+        return _count(topo.mask(src, core))
+
+    def wait_unit(q, u):
+        if side is not None and u // 8 == side:
+            q.wait_ge(S["ld%d" % u], 32)
+        else:
+            q.wait_ge(S["w%d" % u], arrival(u))
+
+    def pass_unit(u):
+        wait_unit(g, u)
+        r = _route(u)
+        p = r.index(chip_i) + 1 if chip_i else 0
+        if p < len(r):
+            nxt = _owner(team, u, r[p])
+            send([(unit(u), unit(u), [nxt], topo.mask(core, nxt), S["w%d" % u])])
+        others = [c for c in mine if c != core and not (c in ranks and ranks.index(c) == u // 8)]
+        send([(unit(u), unit(u), others, on, S["w%d" % u])])
+
+    def pass_tokens():
+        dst = [(team["chips"][k][0] + team["chips"][k][1])[wi] for k in range(1, NH + 1)]
+        ms = _split(topo.mask(core, dst[0]), NH)
+        g.wait_ge(S.mg1, 1)
+        send([(T.xm[:, NS * k:NS * (k + 1)], T.xm[:, 0:NS], [dst[k]], ms[k], S.tkh) for k in range(NH)])
+
+    v, s, t, y = g.vector, g.scalar, g.tensor, g.sync
+    nv = [0]
+
+    def did_v(ins):
+        ins.then_inc(S.vs, 1)
+        nv[0] += 1
+
+    def join():
+        v.wait_ge(S.vs, nv[0])
+
+    own_units = [u for u in _order(chip_i) if _owner(team, u, chip_i) == core]
+
+    if side is not None:
+        y.dma_start(T.ki[:], T.keep[:]).then_inc(S.kd, 16)
+        s.dma_start(T.xw[:, 0:2048], T.x[:]).then_inc(S.xd, 16)
+        for ul in range(8):
+            u = 8 * side + ul
+            q = y if ul % 2 == 0 else s
+            q.dma_start(T.wb[:, UW * u:UW * u + 256], T.w1[:, 256 * u:256 * u + 256]).then_inc(S["ld%d" % u], 16)
+            q.dma_start(T.wb[:, UW * u + 256:UW * u + 512], T.w2[:, 256 * u:256 * u + 256]).then_inc(S["ld%d" % u], 16)
+
+        fl = {"allow_small_or_imprecise_dtypes": True}
+        g.iota(I("pid"), [[1, 1]], 0, 1).then_inc(S.io1, 1)
+        g.iota(T.fdiff[:], [[1, 128]], 0, -1, **fl).then_inc(S.io2, 1)
+        g.iota(T.dump[:], [[1, 16]], 4096, 16, **fl).then_inc(S.io2, 1)
+        g.iota(T.fa[:], [[16, 16], [1, 2], [0, 8]], 0, 0, **fl).then_inc(S.io2, 1)
+        g.iota(T.fb[:], [[0, 16], [0, 2], [1, 8]], 0, 0, **fl).then_inc(S.io2, 1)
+        g.iota(T.fsel[:], [[0, 9], [1, 16]], 0, 0, **fl).then_inc(S.io2, 1)
+        g.iota(T.c16[:], [[16, 16]], 0, 0, **fl).then_inc(S.io2, 1)
+
+        did_v(v.memset(T.win[:, 0:2048], 0.0))
+        did_v(v.memset(T.xw[:, 2048:RB], 0.0))
+        did_v(v.memset(T.ones[:], 1.0))
+        v.wait_ge(S.io1, 1)
+        did_v(v.tensor_scalar(I("ri"), I("pid"), 15, None, Op.bitwise_and))
+        did_v(v.tensor_scalar(I("g2i"), I("pid"), 3, 30, Op.logical_shift_right, Op.bitwise_and))
+        did_v(v.tensor_scalar(I("q7i"), I("pid"), 7, None, Op.bitwise_and))
+        did_v(v.tensor_scalar(I("q3i"), I("pid"), 3, None, Op.logical_shift_right))
+        join()
+        v.wait_ge(S.io2, 6)
+        did_v(v.tensor_scalar(C("m0"), I("ri"), 0.0, None, Op.is_equal))
+        did_v(v.tensor_scalar(C("m1"), I("ri"), 1.0, None, Op.is_equal))
+        did_v(v.tensor_scalar(C("m2"), I("ri"), 2.0, None, Op.is_equal))
+        did_v(v.tensor_scalar(C("m23"), I("ri"), 2.0, None, Op.is_ge))
+        did_v(v.tensor_scalar(C("w3"), I("ri"), 3.0, -2048.0, Op.is_equal, Op.mult))
+        did_v(v.tensor_copy(C("g2f"), I("g2i")))
+        did_v(v.tensor_copy(C("q7f"), I("q7i")))
+        did_v(v.tensor_copy(C("q3f"), I("q3i")))
+        did_v(v.tensor_scalar(T.tri[:], T.fdiff[:], 0.0, 1.0 if side == 0 else -1.0,
+                              Op.is_gt if side == 0 else Op.is_lt, Op.mult))
+        did_v(v.tensor_scalar(T.cz[:], T.dump[:], -1.0, -1.0 if side == 0 else 2048.0, Op.mult, Op.add))
+        join()
+        did_v(v.tensor_scalar(C("w01"), C("m1"), 256.0, C("m0"), Op.mult, Op.add))
+        did_v(v.tensor_tensor(C("w2c"), C("m2"), C("g2f"), Op.mult))
+        did_v(v.tensor_scalar(T.fc[:], T.fa[:], C("m0"), C("m23"), Op.mult, Op.add))
+        did_v(v.tensor_scalar(T.fd[:], T.fb[:], C("m1"), None, Op.mult))
+        did_v(v.tensor_scalar(C("tcol"), C("q7f"), 256.0, C("q3f"), Op.mult, Op.add))
+        join()
+        did_v(v.tensor_tensor(C("wa"), C("w01"), C("w2c"), Op.add))
+        did_v(v.tensor_tensor(T.vals[:], T.fc[:], T.fd[:], Op.add))
+        join()
+        did_v(v.tensor_tensor(C("wc"), C("wa"), C("w3"), Op.add))
+        v.wait_ge(S.kd, 16)
+        did_v(v.tensor_copy(T.kf[:], T.ki[:]))
+        join()
+        did_v(v.tensor_tensor_scan(T.scn[:], T.ones[:], T.kf[:], 0.0, Op.mult, Op.add))
+        join()
+        t.wait_ge(S.vs, nv[0])
+        t.matmul(T.h5[:, 0:1], T.tri[:], T.scn[:, 15:16], True, True).then_inc(S.tm, 1)
+        if side == 0:
+            did_v(v.tensor_tensor(T.pa[:], T.cz[:], T.scn[:], Op.add))
+        else:
+            did_v(v.tensor_tensor(T.pa[:], T.cz[:], T.scn[:], Op.subtract))
+        did_v(v.tensor_scalar(T.zsel[:], T.fsel[:], 15.0, C("wc"), Op.is_equal, Op.mult))
+        join()
+        did_v(v.tensor_tensor(T.pb[:], T.pa[:], T.kf[:], Op.mult))
+        join()
+        did_v(v.tensor_tensor(T.pp[:], T.pb[:], T.dump[:], Op.add))
+        join()
+        v.wait_ge(S.tm, 1)
+        did_v(v.tensor_scalar(T.offs[:], T.pp[:], T.h5[:, 0:1], None, Op.add))
+        join()
+        did_v(v.tensor_copy(T.win[:, 0:WMAX].indirect(T.offs[:, 0:16]), T.vals[:]))
+        t.wait_ge(S.vs, nv[0])
+        for half, bank, sem in ((0, T.h3, S.tx), (1, T.h4, S.ty)):
+            for r in range(16):
+                ins = t.matmul(bank[:, 0:64], T.zsel[:, 15 - r:143 - r],
+                               T.win[:, 1024 * half + r:1024 * half + 1024:16], r == 0, r == 15)
+                if r == 15:
+                    ins.then_inc(sem, 1)
+        for half, bank, sem, lst in ((0, T.h3, S.tx, T.listx), (1, T.h4, S.ty, T.listy)):
+            v.wait_ge(sem, 1)
+            did_v(v.tensor_scalar(lst[:], bank[:, 0:64], 2048.0, None, Op.add))
+            join()
+            s.wait_ge(S.vs, nv[0])
+            if half == 0:
+                v.wait_ge(S.xd, 16)
+                s.wait_ge(S.xd, 16)
+            b = 1024 * half
+            did_v(v.tensor_copy(T.xg[:, b:b + 512], T.xw[:, 0:RB].indirect(lst[:, 0:32])))
+            s.activation(T.xg[:, b + 512:b + 1024], T.xw[:, 0:RB].indirect(lst[:, 32:64]), Act.Copy).then_inc(S.sg, 1)
+            if half == 0:
+                after_x = nv[0]
+            else:
+                after_y = nv[0]
+
+        def hand_out(k):
+            ms = _split(on, 2)
+            us = [8 * side + 2 * k, 8 * side + 2 * k + 1]
+            for u in us:
+                g.wait_ge(S["ld%d" % u], 32)
+            send([(unit(u), unit(u), [_owner(team, u, 0)], ms[i], S["w%d" % u]) for i, u in enumerate(us)])
+
+        hand_out(0)
+        hand_out(1)
+        land, lsem = (T.ta, S.tka) if side == 0 else (T.tb, S.tkb)
+        for half in range(2):
+            ms = _split(on, 4)
+            g.wait_ge(S.vs, (after_x, after_y)[half])
+            g.wait_ge(S.sg, half + 1)
+            send([(T.xg[:, 256 * w:256 * (w + 1)], land[:], [home[w]], ms[w % 4], lsem)
+                  for w in range(4 * half, 4 * half + 4) if home[w] != core])
+
+        did_v(v.tensor_scalar(T.tq[:], T.c16[:], C("tcol"), None, Op.add))
+        did_v(v.tensor_scalar(T.ga[:], T.pp[:], T.h5[:, 0:1], None, Op.add))
+        join()
+        did_v(v.tensor_scalar(T.tqm[:], T.tq[:], -1.0, float(RB), Op.mult, Op.add))
+        join()
+        did_v(v.tensor_tensor(T.gb[:], T.ga[:], T.tqm[:], Op.add))
+        join()
+        did_v(v.tensor_tensor(T.gd[:], T.gb[:], T.kf[:], Op.mult))
+        join()
+        did_v(v.tensor_tensor(T.ge[:], T.gd[:], T.tq[:], Op.add))
+        join()
+        did_v(v.tensor_copy(T.ysrc[:], T.ge[:]))
+        y.wait_ge(S.vs, nv[0])
+        y.dma_start(T.ydram[:], T.ysrc[:]).then_inc(S.yl1, 16)
+        y.wait_ge(S.yl1, 16)
+        for k in range(8):
+            y.dma_start(T.ylist[16 * k:16 * k + 16, :], T.ydram[:]).then_inc(S.yl2, 16)
+
+    if chip_i == 0:
+        pa, pb = T.ta, T.tb
+        oa = ob = 0
+        if side == 0:
+            pa, oa = T.xg, 256 * wi
+        if side == 1:
+            pb, ob = T.xg, 256 * wi
+        if side is not None:
+            v.wait_ge(S.vs, nv[0])
+            v.wait_ge(S.sg, 2)
+            t.wait_ge(S.vs, nv[0])
+        if side != 0:
+            v.wait_ge(S.tka, _count(_split(on, 4)[0]))
+        if side != 1:
+            v.wait_ge(S.tkb, _count(_split(on, 4)[0]))
+        cut = NH * NS
+        v.tensor_tensor(T.xm[:, 0:cut], pa[:, oa:oa + cut], pb[:, ob:ob + cut], Op.add).then_inc(S.mg1, 1)
+        v.tensor_tensor(T.xm[:, cut:256], pa[:, oa + cut:oa + 256], pb[:, ob + cut:ob + 256], Op.add).then_inc(S.mg2, 1)
+
+    if side is not None:
+        hand_out(2)
+        pass_tokens()
+        hand_out(3)
+    elif chip_i == 0:
+        for u in own_units:
+            if u % 8 < 4:
+                pass_unit(u)
+        pass_tokens()
+        for u in own_units:
+            if u % 8 >= 4:
+                pass_unit(u)
+    else:
+        for u in own_units:
+            pass_unit(u)
+
+    xo = first if chip_i == 0 else 0
+    x_in = T.xm[:, xo:xo + n]
+    if chip_i == 0:
+        t.wait_ge(S.mg2, 1)
+    else:
+        ms = _split(topo.mask(home[wi], core), NH)
+        t.wait_ge(S.tkh, _count(ms[chip_i - 1]))
+    order = _order(chip_i)
+
+    def layer1(i):
+        u = order[i]
+        wait_unit(t, u)
+        for j in range(2):
+            t.matmul(T["h%d" % (i % NB)][:, j * n:(j + 1) * n], T.wb[:, UW * u + 128 * j:UW * u + 128 * (j + 1)],
+                     x_in, True, True).then_inc(S["l%d" % i], 1)
+        s.wait_ge(S["l%d" % i], 2)
+        s.activation(T.hb[:, 256 * i:256 * i + 2 * n], T["h%d" % (i % NB)][:, 0:2 * n], Act.Relu).then_inc(S["r%d" % i], 1)
+
+    def layer2(i):
+        u = order[i]
+        t.wait_ge(S["r%d" % i], 1)
+        for j in range(2):
+            last = i == NU - 1 and j == 1
+            ins = t.matmul(T.yacc[:, 0:n], T.wb[:, UW * u + 256 + 128 * j:UW * u + 384 + 128 * j],
+                           T.hb[:, 256 * i + n * j:256 * i + n * (j + 1)], i == 0 and j == 0, last)
+            if last:
+                ins.then_inc(S.yd, 1)
+
+    for i in range(NU + 2):
+        if i < NU:
+            layer1(i)
+        if i >= 2:
+            layer2(i - 2)
+
+    slot = RB + 256 * wi + first
+    target = T.xw[:, slot:slot + n]
+    out = target if side is not None else T.yo[:, 0:n]
+    v.wait_ge(S.yd, 1)
+    v.tensor_copy(out, T.yacc[:, 0:n]).then_inc(S.yc, 1)
+    g.wait_ge(S.yc, 1)
+    dst = [c for c in ranks if c != core]
+    send([(out, target, dst, topo.mask(core, dst[0]), S.res)])
+
+    if side is not None:
+        total = 0
+        for ci, hv in enumerate(team["chips"]):
+            for c in hv[0] + hv[1]:
+                if c != core:
+                    total += _count(topo.mask(c, core))
+        for q in (v, s):
+            q.wait_ge(S.yl2, 128)
+            q.wait_ge(S.yc, 1)
+            q.wait_ge(S.res, total)
+        allx = T.xw[:, 0:RB + 2048]
+        for k in range(2):
+            a, b = 1024 * k, 1024 * k + 512
+            v.tensor_copy(T.yb[:, a:a + 512], allx.indirect(T.ylist[:, a // 16:a // 16 + 32])).then_inc(S.fv, 1)
+            s.activation(T.yb[:, b:b + 512], allx.indirect(T.ylist[:, b // 16:b // 16 + 32]), Act.Copy).then_inc(S.fs, 1)
+        for k in range(2):
+            a, b = 1024 * k, 1024 * k + 512
+            y.wait_ge(S.fv, k + 1)
+            y.dma_start(T.y[:, a:a + 512], T.yb[:, a:a + 512]).then_inc(S.ys, 16)
+            q, sem = (y, S.ys) if k == 0 else (s, S.yt)
+            q.wait_ge(S.fs, k + 1)
+            q.dma_start(T.y[:, b:b + 512], T.yb[:, b:b + 512]).then_inc(sem, 16)
+        y.wait_ge(S.ys, 48)
+        s.wait_ge(S.yt, 16)
+    g.wait_ge(S.loc, loc[0])

@@ -3,16 +3,22 @@ from concourse.bass import DstId, RemoteDMATransfer
 from concourse.mybir import dt, AluOpType as Op, AxisListType, ActivationFunctionType as Act
 
 NH = 2
-NS = 72
+NS = 76
+PRE = 2
+OP = 4
+HOME_HI = True
+HELP_HI = False
 NCORES = 96
 NU = 16
 UW = 512
+XB = 4
 RB = 2052
 NB = 6
 WMAX = 8192
+CUTS = (0, 256, 640, 1024)
 
 INTS = ("pid", "ri", "g2i", "q7i", "q3i")
-COLS = ("m0", "m1", "m2", "m23", "w3", "g2f", "q7f", "q3f", "w01", "w2c", "wa", "wc", "tcol")
+COLS = ("m0", "m1", "m2", "g2f", "q7f", "q3f", "w01", "wc", "tcol")
 SCRATCH = {
     "cint": ("sbuf", [128, 8], "int32"),
     "cflt": ("sbuf", [128, 16], "float32"),
@@ -62,8 +68,8 @@ SCRATCH = {
 for _n in range(NB):
     SCRATCH["h%d" % _n] = ("psum", [128, 512], "float32")
 
-SEMAPHORES = ["io1", "io2", "vs", "sg", "tm", "tx", "ty", "kd", "xd", "tka", "tkb", "tkh", "mg1", "mg2", "yd", "yc",
-              "res", "loc", "yl1", "yl2", "fv", "fs", "ys", "yt"]
+SEMAPHORES = ["io1", "io2", "io3", "io4", "io5", "vs", "sc", "sg", "tm", "tx", "ty", "kq", "kd", "xd", "tka", "tkb",
+              "tkh", "mg1", "mg2", "yd", "yc", "res", "loc", "yl1", "yl2", "fv", "fs", "ys", "yt"]
 SEMAPHORES += ["w%d" % u for u in range(NU)] + ["ld%d" % u for u in range(NU)]
 SEMAPHORES += ["l%d" % u for u in range(NU)] + ["r%d" % u for u in range(NU)]
 
@@ -116,16 +122,40 @@ def _pos(u, ci):
     return 0 if ci == 0 else 1 + _route(u).index(ci)
 
 
+def _reach(u, ci):
+    ul = u % 8
+    return ul // 2 * 2 + (2 if ul >= 2 * PRE else 0) + 4.5 * _pos(u, ci)
+
+
 def _order(ci):
-    def key(u):
-        ul = u % 8
-        return (ul // 2 * 2 + (3 if ul >= 4 else 0) + 4 * _pos(u, ci), ul, u)
-    return sorted(range(NU), key=key)
+    return sorted(range(NU), key=lambda u: (_reach(u, ci), u % 8, u))
 
 
 def _owner(team, u, ci):
     s, ul = u // 8, u % 8
     return team["chips"][ci][s][1 + ul % 3] if ci == 0 else team["chips"][ci][s][ul % 4]
+
+
+def _expected(team):
+    exp = {c: {} for hv in team["chips"] for c in hv[0] + hv[1]}
+    for ci, hv in enumerate(team["chips"]):
+        mine = hv[0] + hv[1]
+        step = 1.1 if ci == 0 and HOME_HI else 0.55
+        free = {c: 0.0 for c in mine}
+        for u in _order(ci):
+            own = _owner(team, u, ci)
+            a = _reach(u, ci)
+            exp[own][u] = a
+            k = mine.index(own)
+            t = max(free[own], a + 2)
+            for c in mine[k + 1:] + mine[:k]:
+                if ci == 0 and c == hv[u // 8][0]:
+                    exp[c][u] = u % 8 - 10
+                else:
+                    t += step
+                    exp[c][u] = t
+            free[own] = t
+    return exp
 
 
 def rank_program(g, core, T, topo):
@@ -145,6 +175,8 @@ def rank_program(g, core, T, topo):
     first = NH * NS if chip_i == 0 else (chip_i - 1) * NS
     S = T.sem
     on = topo.mask(core, [c for c in mine if c != core][0])
+    away = topo.mask(core, team["chips"][1 if chip_i == 0 else 0][0][1])
+    spread_mask = on & ~away if (HOME_HI if chip_i == 0 else HELP_HI) else on
     loc = [0]
 
     def I(name):
@@ -171,7 +203,7 @@ def rank_program(g, core, T, topo):
     def arrival(u):
         own = _owner(team, u, chip_i)
         if core != own:
-            return _count(on)
+            return _count(spread_mask)
         if chip_i == 0:
             return _count(_split(on, 2)[0])
         r = _route(u)
@@ -192,12 +224,13 @@ def rank_program(g, core, T, topo):
         if p < len(r):
             nxt = _owner(team, u, r[p])
             send([(unit(u), unit(u), [nxt], topo.mask(core, nxt), S["w%d" % u])])
-        others = [c for c in mine if c != core and not (c in ranks and ranks.index(c) == u // 8)]
-        send([(unit(u), unit(u), others, on, S["w%d" % u])])
+        around = mine[wi + 1:] + mine[:wi]
+        others = [c for c in around if not (c in ranks and ranks.index(c) == u // 8)]
+        send([(unit(u), unit(u), others, spread_mask, S["w%d" % u])])
 
     def pass_tokens():
         dst = [(team["chips"][k][0] + team["chips"][k][1])[wi] for k in range(1, NH + 1)]
-        ms = _split(topo.mask(core, dst[0]), NH)
+        ms = _split(away, NH)
         g.wait_ge(S.mg1, 1)
         send([(T.xm[:, NS * k:NS * (k + 1)], T.xm[:, 0:NS], [dst[k]], ms[k], S.tkh) for k in range(NH)])
 
@@ -214,76 +247,79 @@ def rank_program(g, core, T, topo):
     own_units = [u for u in _order(chip_i) if _owner(team, u, chip_i) == core]
 
     if side is not None:
-        y.dma_start(T.ki[:], T.keep[:]).then_inc(S.kd, 16)
-        s.dma_start(T.xw[:, 0:2048], T.x[:]).then_inc(S.xd, 16)
-        for ul in range(8):
+        def load(q, ul):
             u = 8 * side + ul
-            q = y if ul % 2 == 0 else s
             q.dma_start(T.wb[:, UW * u:UW * u + 256], T.w1[:, 256 * u:256 * u + 256]).then_inc(S["ld%d" % u], 16)
             q.dma_start(T.wb[:, UW * u + 256:UW * u + 512], T.w2[:, 256 * u:256 * u + 256]).then_inc(S["ld%d" % u], 16)
+
+        y.dma_start(T.ki[:], T.keep[:]).then_inc(S.kd, 16)
+        y.sem_inc(S.kq, 1)
+        s.wait_ge(S.kq, 1)
+        load(y, 0)
+        load(s, 1)
+        load(y, 2)
+        s.dma_start(T.xw[:, XB:RB], T.x[:]).then_inc(S.xd, 16)
+        load(y, 3)
+        for ul in range(4, 8):
+            y.wait_ge(S["ld%d" % (8 * side + ul - 2)], 32)
+            load(y, ul)
 
         fl = {"allow_small_or_imprecise_dtypes": True}
         g.iota(I("pid"), [[1, 1]], 0, 1).then_inc(S.io1, 1)
         g.iota(T.fdiff[:], [[1, 128]], 0, -1, **fl).then_inc(S.io2, 1)
-        g.iota(T.dump[:], [[1, 16]], 4096, 16, **fl).then_inc(S.io2, 1)
-        g.iota(T.fa[:], [[16, 16], [1, 2], [0, 8]], 0, 0, **fl).then_inc(S.io2, 1)
-        g.iota(T.fb[:], [[0, 16], [0, 2], [1, 8]], 0, 0, **fl).then_inc(S.io2, 1)
-        g.iota(T.fsel[:], [[0, 9], [1, 16]], 0, 0, **fl).then_inc(S.io2, 1)
-        g.iota(T.c16[:], [[16, 16]], 0, 0, **fl).then_inc(S.io2, 1)
+        g.iota(T.fa[:], [[16, 16], [1, 2], [0, 8]], XB, 0, **fl).then_inc(S.io3, 1)
+        g.iota(T.fb[:], [[0, 16], [0, 2], [1, 8]], 0, 0, **fl).then_inc(S.io3, 1)
+        g.iota(T.dump[:], [[1, 16]], 4096, 16, **fl).then_inc(S.io4, 1)
+        if side == 0:
+            g.iota(T.cz[:], [[-1, 16]], -1 - 4096, -16, **fl).then_inc(S.io4, 1)
+        else:
+            g.iota(T.cz[:], [[-1, 16]], 2048 - 4096, -16, **fl).then_inc(S.io4, 1)
+        g.iota(T.fsel[:], [[0, 9], [1, 16]], 0, 0, **fl).then_inc(S.io5, 1)
+        g.iota(T.c16[:], [[16, 16]], XB, 0, **fl).then_inc(S.io5, 1)
 
         did_v(v.memset(T.win[:, 0:2048], 0.0))
-        did_v(v.memset(T.xw[:, 2048:RB], 0.0))
+        did_v(v.memset(T.xw[:, 0:XB], 0.0))
         did_v(v.memset(T.ones[:], 1.0))
         v.wait_ge(S.io1, 1)
         did_v(v.tensor_scalar(I("ri"), I("pid"), 15, None, Op.bitwise_and))
         did_v(v.tensor_scalar(I("g2i"), I("pid"), 3, 30, Op.logical_shift_right, Op.bitwise_and))
-        did_v(v.tensor_scalar(I("q7i"), I("pid"), 7, None, Op.bitwise_and))
-        did_v(v.tensor_scalar(I("q3i"), I("pid"), 3, None, Op.logical_shift_right))
         join()
-        v.wait_ge(S.io2, 6)
         did_v(v.tensor_scalar(C("m0"), I("ri"), 0.0, None, Op.is_equal))
         did_v(v.tensor_scalar(C("m1"), I("ri"), 1.0, None, Op.is_equal))
         did_v(v.tensor_scalar(C("m2"), I("ri"), 2.0, None, Op.is_equal))
-        did_v(v.tensor_scalar(C("m23"), I("ri"), 2.0, None, Op.is_ge))
-        did_v(v.tensor_scalar(C("w3"), I("ri"), 3.0, -2048.0, Op.is_equal, Op.mult))
         did_v(v.tensor_copy(C("g2f"), I("g2i")))
-        did_v(v.tensor_copy(C("q7f"), I("q7i")))
-        did_v(v.tensor_copy(C("q3f"), I("q3i")))
+        join()
+        s.wait_ge(S.vs, nv[0])
+        s.wait_ge(S.io3, 2)
+        s.activation(T.fc[:], T.fa[:], Act.Identity, bias=C("m2"), scale=C("m0")).then_inc(S.sc, 1)
+        s.activation(T.fd[:], T.fb[:], Act.Identity, scale=C("m1")).then_inc(S.sc, 1)
+        v.wait_ge(S.io2, 1)
+        did_v(v.tensor_scalar(C("w01"), C("m1"), 256.0, C("m0"), Op.mult, Op.add))
         did_v(v.tensor_scalar(T.tri[:], T.fdiff[:], 0.0, 1.0 if side == 0 else -1.0,
                               Op.is_gt if side == 0 else Op.is_lt, Op.mult))
-        did_v(v.tensor_scalar(T.cz[:], T.dump[:], -1.0, -1.0 if side == 0 else 2048.0, Op.mult, Op.add))
-        join()
-        did_v(v.tensor_scalar(C("w01"), C("m1"), 256.0, C("m0"), Op.mult, Op.add))
-        did_v(v.tensor_tensor(C("w2c"), C("m2"), C("g2f"), Op.mult))
-        did_v(v.tensor_scalar(T.fc[:], T.fa[:], C("m0"), C("m23"), Op.mult, Op.add))
-        did_v(v.tensor_scalar(T.fd[:], T.fb[:], C("m1"), None, Op.mult))
-        did_v(v.tensor_scalar(C("tcol"), C("q7f"), 256.0, C("q3f"), Op.mult, Op.add))
-        join()
-        did_v(v.tensor_tensor(C("wa"), C("w01"), C("w2c"), Op.add))
-        did_v(v.tensor_tensor(T.vals[:], T.fc[:], T.fd[:], Op.add))
-        join()
-        did_v(v.tensor_tensor(C("wc"), C("wa"), C("w3"), Op.add))
         v.wait_ge(S.kd, 16)
         did_v(v.tensor_copy(T.kf[:], T.ki[:]))
         join()
         did_v(v.tensor_tensor_scan(T.scn[:], T.ones[:], T.kf[:], 0.0, Op.mult, Op.add))
+        did_v(v.tensor_scalar(C("wc"), C("g2f"), C("m2"), C("w01"), Op.mult, Op.add))
         join()
         t.wait_ge(S.vs, nv[0])
         t.matmul(T.h5[:, 0:1], T.tri[:], T.scn[:, 15:16], True, True).then_inc(S.tm, 1)
-        if side == 0:
-            did_v(v.tensor_tensor(T.pa[:], T.cz[:], T.scn[:], Op.add))
-        else:
-            did_v(v.tensor_tensor(T.pa[:], T.cz[:], T.scn[:], Op.subtract))
-        did_v(v.tensor_scalar(T.zsel[:], T.fsel[:], 15.0, C("wc"), Op.is_equal, Op.mult))
+        v.wait_ge(S.io4, 2)
+        did_v(v.tensor_tensor(T.pa[:], T.cz[:], T.scn[:], Op.add if side == 0 else Op.subtract))
         join()
         did_v(v.tensor_tensor(T.pb[:], T.pa[:], T.kf[:], Op.mult))
         join()
         did_v(v.tensor_tensor(T.pp[:], T.pb[:], T.dump[:], Op.add))
+        v.wait_ge(S.sc, 2)
+        did_v(v.tensor_tensor(T.vals[:], T.fc[:], T.fd[:], Op.add))
         join()
         v.wait_ge(S.tm, 1)
         did_v(v.tensor_scalar(T.offs[:], T.pp[:], T.h5[:, 0:1], None, Op.add))
         join()
         did_v(v.tensor_copy(T.win[:, 0:WMAX].indirect(T.offs[:, 0:16]), T.vals[:]))
+        v.wait_ge(S.io5, 2)
+        did_v(v.tensor_scalar(T.zsel[:], T.fsel[:], 15.0, C("wc"), Op.is_equal, Op.mult))
         t.wait_ge(S.vs, nv[0])
         for half, bank, sem in ((0, T.h3, S.tx), (1, T.h4, S.ty)):
             for r in range(16):
@@ -291,9 +327,10 @@ def rank_program(g, core, T, topo):
                                T.win[:, 1024 * half + r:1024 * half + 1024:16], r == 0, r == 15)
                 if r == 15:
                     ins.then_inc(sem, 1)
+        after = []
         for half, bank, sem, lst in ((0, T.h3, S.tx, T.listx), (1, T.h4, S.ty, T.listy)):
             v.wait_ge(sem, 1)
-            did_v(v.tensor_scalar(lst[:], bank[:, 0:64], 2048.0, None, Op.add))
+            did_v(v.tensor_copy(lst[:], bank[:, 0:64]))
             join()
             s.wait_ge(S.vs, nv[0])
             if half == 0:
@@ -302,10 +339,7 @@ def rank_program(g, core, T, topo):
             b = 1024 * half
             did_v(v.tensor_copy(T.xg[:, b:b + 512], T.xw[:, 0:RB].indirect(lst[:, 0:32])))
             s.activation(T.xg[:, b + 512:b + 1024], T.xw[:, 0:RB].indirect(lst[:, 32:64]), Act.Copy).then_inc(S.sg, 1)
-            if half == 0:
-                after_x = nv[0]
-            else:
-                after_y = nv[0]
+            after.append(nv[0])
 
         def hand_out(k):
             ms = _split(on, 2)
@@ -314,18 +348,26 @@ def rank_program(g, core, T, topo):
                 g.wait_ge(S["ld%d" % u], 32)
             send([(unit(u), unit(u), [_owner(team, u, 0)], ms[i], S["w%d" % u]) for i, u in enumerate(us)])
 
-        hand_out(0)
-        hand_out(1)
+        for k in range(PRE):
+            hand_out(k)
         land, lsem = (T.ta, S.tka) if side == 0 else (T.tb, S.tkb)
         for half in range(2):
             ms = _split(on, 4)
-            g.wait_ge(S.vs, (after_x, after_y)[half])
+            g.wait_ge(S.vs, after[half])
             g.wait_ge(S.sg, half + 1)
             send([(T.xg[:, 256 * w:256 * (w + 1)], land[:], [home[w]], ms[w % 4], lsem)
                   for w in range(4 * half, 4 * half + 4) if home[w] != core])
 
-        did_v(v.tensor_scalar(T.tq[:], T.c16[:], C("tcol"), None, Op.add))
+        did_v(v.tensor_scalar(I("q7i"), I("pid"), 7, None, Op.bitwise_and))
+        did_v(v.tensor_scalar(I("q3i"), I("pid"), 3, None, Op.logical_shift_right))
         did_v(v.tensor_scalar(T.ga[:], T.pp[:], T.h5[:, 0:1], None, Op.add))
+        join()
+        did_v(v.tensor_copy(C("q7f"), I("q7i")))
+        did_v(v.tensor_copy(C("q3f"), I("q3i")))
+        join()
+        did_v(v.tensor_scalar(C("tcol"), C("q7f"), 256.0, C("q3f"), Op.mult, Op.add))
+        join()
+        did_v(v.tensor_scalar(T.tq[:], T.c16[:], C("tcol"), None, Op.add))
         join()
         did_v(v.tensor_scalar(T.tqm[:], T.tq[:], -1.0, float(RB), Op.mult, Op.add))
         join()
@@ -367,11 +409,11 @@ def rank_program(g, core, T, topo):
         hand_out(3)
     elif chip_i == 0:
         for u in own_units:
-            if u % 8 < 4:
+            if u % 8 < OP:
                 pass_unit(u)
         pass_tokens()
         for u in own_units:
-            if u % 8 >= 4:
+            if u % 8 >= OP:
                 pass_unit(u)
     else:
         for u in own_units:
@@ -384,7 +426,8 @@ def rank_program(g, core, T, topo):
     else:
         ms = _split(topo.mask(home[wi], core), NH)
         t.wait_ge(S.tkh, _count(ms[chip_i - 1]))
-    order = _order(chip_i)
+    exp = _expected(team)[core]
+    order = sorted(range(NU), key=lambda u: exp[u])
 
     def layer1(i):
         u = order[i]
@@ -431,17 +474,16 @@ def rank_program(g, core, T, topo):
             q.wait_ge(S.yc, 1)
             q.wait_ge(S.res, total)
         allx = T.xw[:, 0:RB + 2048]
-        for k in range(2):
-            a, b = 1024 * k, 1024 * k + 512
-            v.tensor_copy(T.yb[:, a:a + 512], allx.indirect(T.ylist[:, a // 16:a // 16 + 32])).then_inc(S.fv, 1)
-            s.activation(T.yb[:, b:b + 512], allx.indirect(T.ylist[:, b // 16:b // 16 + 32]), Act.Copy).then_inc(S.fs, 1)
-        for k in range(2):
-            a, b = 1024 * k, 1024 * k + 512
-            y.wait_ge(S.fv, k + 1)
-            y.dma_start(T.y[:, a:a + 512], T.yb[:, a:a + 512]).then_inc(S.ys, 16)
-            q, sem = (y, S.ys) if k == 0 else (s, S.yt)
-            q.wait_ge(S.fs, k + 1)
-            q.dma_start(T.y[:, b:b + 512], T.yb[:, b:b + 512]).then_inc(sem, 16)
-        y.wait_ge(S.ys, 48)
+        for a, b in zip(CUTS, CUTS[1:]):
+            for q, o, sem in ((v, 0, S.fv), (s, 1024, S.fs)):
+                to, src = T.yb[:, o + a:o + b], allx.indirect(T.ylist[:, (o + a) // 16:(o + b) // 16])
+                ins = q.tensor_copy(to, src) if q is v else q.activation(to, src, Act.Copy)
+                ins.then_inc(sem, 1)
+        for k in range(3):
+            a, b = CUTS[k], CUTS[k + 1]
+            for q, o, sem, end in ((y, 0, S.fv, S.ys), (s if k == 2 else y, 1024, S.fs, S.yt if k == 2 else S.ys)):
+                q.wait_ge(sem, k + 1)
+                q.dma_start(T.y[:, o + a:o + b], T.yb[:, o + a:o + b]).then_inc(end, 16)
+        y.wait_ge(S.ys, 80)
         s.wait_ge(S.yt, 16)
     g.wait_ge(S.loc, loc[0])

@@ -3,13 +3,15 @@ from concourse.bass import DstId, RemoteDMATransfer
 from concourse.mybir import dt, AluOpType as Op, AxisListType, ActivationFunctionType as Act
 
 NH = 2
-NS = 76
+NS = 64
 PRE = 2
 OP = 4
-HOME_HI = True
-HELP_HI = False
+LG = 2
+HS = 1
+EARLY = 4
+TAIL = 4
 NCORES = 96
-NU = 16
+NU = 8
 UW = 512
 XB = 4
 RB = 2052
@@ -28,8 +30,11 @@ SCRATCH = {
     "ta": ("sbuf", [128, 256], "float32"),
     "tb": ("sbuf", [128, 256], "float32"),
     "xm": ("sbuf", [128, 256], "float32"),
-    "hb": ("sbuf", [128, NU * 256], "float32"),
-    "yo": ("sbuf", [128, 256], "float32"),
+    "x2": ("sbuf", [128, 256], "float32"),
+    "hb": ("sbuf", [128, NU * 512], "float32"),
+    "po": ("sbuf", [128, 128], "float32"),
+    "rp": ("sbuf", [128, 128], "float32"),
+    "yo": ("sbuf", [128, 128], "float32"),
     "yb": ("sbuf", [128, 2048], "float32"),
     "win": ("sbuf", [128, WMAX], "bfloat16"),
     "vals": ("sbuf", [128, 256], "bfloat16"),
@@ -63,15 +68,15 @@ SCRATCH = {
     "listy": ("sbuf", [128, 64], "uint16"),
     "ylist": ("sbuf", [128, 128], "uint16"),
     "ydram": ("dram", [128, 16], "uint16"),
-    "yacc": ("psum", [128, 512], "float32"),
+    "ya0": ("psum", [128, 512], "float32"),
+    "ya1": ("psum", [128, 512], "float32"),
 }
 for _n in range(NB):
     SCRATCH["h%d" % _n] = ("psum", [128, 512], "float32")
 
 SEMAPHORES = ["io1", "io2", "io3", "io4", "io5", "vs", "sc", "sg", "tm", "tx", "ty", "kq", "kd", "xd", "tka", "tkb",
-              "tkh", "mg1", "mg2", "yd", "yc", "res", "loc", "yl1", "yl2", "fv", "fs", "ys", "yt"]
-SEMAPHORES += ["w%d" % u for u in range(NU)] + ["ld%d" % u for u in range(NU)]
-SEMAPHORES += ["l%d" % u for u in range(NU)] + ["r%d" % u for u in range(NU)]
+              "tkh", "xe", "mg1", "mg2", "yp", "yd", "pc", "rp", "yc", "res", "loc", "yl1", "yl2", "fv", "fs", "ys", "yt"]
+SEMAPHORES += ["%s%d" % (_k, _n) for _k in ("w", "ld", "l", "r") for _n in range(NU)]
 
 
 def _count(mask):
@@ -118,43 +123,37 @@ def _route(u):
     return [1 + (u + i) % NH for i in range(NH)]
 
 
-def _pos(u, ci):
-    return 0 if ci == 0 else 1 + _route(u).index(ci)
-
-
 def _reach(u, ci):
-    ul = u % 8
-    return ul // 2 * 2 + (2 if ul >= 2 * PRE else 0) + 4.5 * _pos(u, ci)
+    pos = 0 if ci == 0 else 1 + _route(u).index(ci)
+    return u // 2 * 2 + (2 if u >= 2 * PRE else 0) + 4.5 * pos
 
 
 def _order(ci):
-    return sorted(range(NU), key=lambda u: (_reach(u, ci), u % 8, u))
+    return sorted(range(NU), key=lambda u: (_reach(u, ci), u))
 
 
-def _owner(team, u, ci):
-    s, ul = u // 8, u % 8
-    return team["chips"][ci][s][1 + ul % 3] if ci == 0 else team["chips"][ci][s][ul % 4]
+def _owner(die, u, ci):
+    return die[1 + u % 3] if ci == 0 else die[u % 4]
 
 
-def _expected(team):
-    exp = {c: {} for hv in team["chips"] for c in hv[0] + hv[1]}
-    for ci, hv in enumerate(team["chips"]):
-        mine = hv[0] + hv[1]
-        step = 1.1 if ci == 0 and HOME_HI else 0.55
-        free = {c: 0.0 for c in mine}
-        for u in _order(ci):
-            own = _owner(team, u, ci)
-            a = _reach(u, ci)
-            exp[own][u] = a
-            k = mine.index(own)
-            t = max(free[own], a + 2)
-            for c in mine[k + 1:] + mine[:k]:
-                if ci == 0 and c == hv[u // 8][0]:
-                    exp[c][u] = u % 8 - 10
-                else:
-                    t += step
-                    exp[c][u] = t
-            free[own] = t
+def _expected(die, ci, core):
+    exp, free = {}, {c: 0.0 for c in die}
+    for u in _order(ci):
+        own = _owner(die, u, ci)
+        a = _reach(u, ci)
+        if core == own:
+            exp[u] = a
+        k = die.index(own)
+        t = max(free[own], a + 2)
+        for c in die[k + 1:] + die[:k]:
+            if ci == 0 and c == die[0]:
+                if core == c:
+                    exp[u] = u - 10
+            else:
+                t += 1.1 if ci == 0 else 0.55
+                if core == c:
+                    exp[u] = t
+        free[own] = t
     return exp
 
 
@@ -170,13 +169,17 @@ def rank_program(g, core, T, topo):
     home = team["chips"][0][0] + team["chips"][0][1]
     mine = team["chips"][chip_i][0] + team["chips"][chip_i][1]
     wi = mine.index(core)
+    hf = wi // 4
+    die = team["chips"][chip_i][hf]
+    peer = mine[(wi + 4) % 8]
     side = ranks.index(core) if core in ranks else None
     n = 256 - NH * NS if chip_i == 0 else NS
+    m = 2 * n
     first = NH * NS if chip_i == 0 else (chip_i - 1) * NS
     S = T.sem
-    on = topo.mask(core, [c for c in mine if c != core][0])
+    on = topo.mask(core, peer)
     away = topo.mask(core, team["chips"][1 if chip_i == 0 else 0][0][1])
-    spread_mask = on & ~away if (HOME_HI if chip_i == 0 else HELP_HI) else on
+    inner = on & ~away if chip_i == 0 else on
     loc = [0]
 
     def I(name):
@@ -192,47 +195,57 @@ def rank_program(g, core, T, topo):
         return DstId(rid=rid, pnc=pid)
 
     def send(parts):
-        g.remote_dma_fused([RemoteDMATransfer(dst_ids=[did(c) for c in ds], dma_engine_mask=m, remote_sem=sem,
-                                              srcs=[src], dsts=[dst] * len(ds)) for src, dst, ds, m, sem in parts],
+        g.remote_dma_fused([RemoteDMATransfer(dst_ids=[did(c) for c in ds], dma_engine_mask=mk, remote_sem=sem,
+                                              srcs=[src], dsts=[dst] * len(ds)) for src, dst, ds, mk, sem in parts],
                            local_sem=S.loc)
         loc[0] += sum(_count(p[3]) for p in parts)
 
     def unit(u):
         return T.wb[:, UW * u:UW * (u + 1)]
 
-    def arrival(u):
-        own = _owner(team, u, chip_i)
-        if core != own:
-            return _count(spread_mask)
-        if chip_i == 0:
-            return _count(_split(on, 2)[0])
-        r = _route(u)
-        p = r.index(chip_i)
-        src = _owner(team, u, r[p - 1] if p else 0)
-        return _count(topo.mask(src, core))
+    def tile(u, layer, j):
+        c = UW * u + 256 * layer + 128 * j
+        return T.wb[:, c:c + 128]
+
+    def part(q):
+        return T.x2[:, n * q:n * q + n]
 
     def wait_unit(q, u):
-        if side is not None and u // 8 == side:
+        if side is not None:
             q.wait_ge(S["ld%d" % u], 32)
+            return
+        if core != _owner(die, u, chip_i):
+            k = _count(inner)
+        elif chip_i == 0:
+            k = _count(_split(on, 2)[0])
         else:
-            q.wait_ge(S["w%d" % u], arrival(u))
+            r = _route(u)
+            p = r.index(chip_i)
+            before = r[p - 1] if p else 0
+            k = _count(topo.mask(_owner(team["chips"][before][hf], u, before), core))
+        q.wait_ge(S["w%d" % u], k)
 
     def pass_unit(u):
         wait_unit(g, u)
         r = _route(u)
         p = r.index(chip_i) + 1 if chip_i else 0
         if p < len(r):
-            nxt = _owner(team, u, r[p])
+            nxt = _owner(team["chips"][r[p]][hf], u, r[p])
             send([(unit(u), unit(u), [nxt], topo.mask(core, nxt), S["w%d" % u])])
-        around = mine[wi + 1:] + mine[:wi]
-        others = [c for c in around if not (c in ranks and ranks.index(c) == u // 8)]
-        send([(unit(u), unit(u), others, spread_mask, S["w%d" % u])])
+        k = die.index(core)
+        others = [c for c in die[k + 1:] + die[:k] if c not in ranks]
+        send([(unit(u), unit(u), others, inner, S["w%d" % u])])
+
+    def swap():
+        send([(part(hf), part(hf), [peer], inner, S.xe)])
 
     def pass_tokens():
         dst = [(team["chips"][k][0] + team["chips"][k][1])[wi] for k in range(1, NH + 1)]
         ms = _split(away, NH)
         g.wait_ge(S.mg1, 1)
-        send([(T.xm[:, NS * k:NS * (k + 1)], T.xm[:, 0:NS], [dst[k]], ms[k], S.tkh) for k in range(NH)])
+        send([(T.xm[:, NS * k:NS * (k + 1)], T.x2[:, NS * hf:NS * hf + NS], [dst[k]], ms[k], S.tkh) for k in range(NH)])
+        g.wait_ge(S.mg2, 1)
+        swap()
 
     v, s, t, y = g.vector, g.scalar, g.tensor, g.sync
     nv = [0]
@@ -244,13 +257,13 @@ def rank_program(g, core, T, topo):
     def join():
         v.wait_ge(S.vs, nv[0])
 
-    own_units = [u for u in _order(chip_i) if _owner(team, u, chip_i) == core]
+    own_units = [u for u in _order(chip_i) if _owner(die, u, chip_i) == core]
 
     if side is not None:
-        def load(q, ul):
-            u = 8 * side + ul
-            q.dma_start(T.wb[:, UW * u:UW * u + 256], T.w1[:, 256 * u:256 * u + 256]).then_inc(S["ld%d" % u], 16)
-            q.dma_start(T.wb[:, UW * u + 256:UW * u + 512], T.w2[:, 256 * u:256 * u + 256]).then_inc(S["ld%d" % u], 16)
+        def load(q, u):
+            c = 256 * (NU * side + u)
+            q.dma_start(T.wb[:, UW * u:UW * u + 256], T.w1[:, c:c + 256]).then_inc(S["ld%d" % u], 16)
+            q.dma_start(T.wb[:, UW * u + 256:UW * u + 512], T.w2[:, c:c + 256]).then_inc(S["ld%d" % u], 16)
 
         y.dma_start(T.ki[:], T.keep[:]).then_inc(S.kd, 16)
         y.sem_inc(S.kq, 1)
@@ -260,9 +273,9 @@ def rank_program(g, core, T, topo):
         load(y, 2)
         s.dma_start(T.xw[:, XB:RB], T.x[:]).then_inc(S.xd, 16)
         load(y, 3)
-        for ul in range(4, 8):
-            y.wait_ge(S["ld%d" % (8 * side + ul - 2)], 32)
-            load(y, ul)
+        for u in range(4, NU):
+            y.wait_ge(S["ld%d" % (u - LG)], 32)
+            load(y, u)
 
         fl = {"allow_small_or_imprecise_dtypes": True}
         g.iota(I("pid"), [[1, 1]], 0, 1).then_inc(S.io1, 1)
@@ -343,10 +356,10 @@ def rank_program(g, core, T, topo):
 
         def hand_out(k):
             ms = _split(on, 2)
-            us = [8 * side + 2 * k, 8 * side + 2 * k + 1]
+            us = [2 * k, 2 * k + 1]
             for u in us:
                 g.wait_ge(S["ld%d" % u], 32)
-            send([(unit(u), unit(u), [_owner(team, u, 0)], ms[i], S["w%d" % u]) for i, u in enumerate(us)])
+            send([(unit(u), unit(u), [_owner(die, u, 0)], ms[i], S["w%d" % u]) for i, u in enumerate(us)])
 
         for k in range(PRE):
             hand_out(k)
@@ -401,71 +414,90 @@ def rank_program(g, core, T, topo):
             v.wait_ge(S.tkb, _count(_split(on, 4)[0]))
         cut = NH * NS
         v.tensor_tensor(T.xm[:, 0:cut], pa[:, oa:oa + cut], pb[:, ob:ob + cut], Op.add).then_inc(S.mg1, 1)
-        v.tensor_tensor(T.xm[:, cut:256], pa[:, oa + cut:oa + 256], pb[:, ob + cut:ob + 256], Op.add).then_inc(S.mg2, 1)
+        v.tensor_tensor(part(hf), pa[:, oa + cut:oa + 256], pb[:, ob + cut:ob + 256], Op.add).then_inc(S.mg2, 1)
 
+    tokens_in = 0
     if side is not None:
         hand_out(2)
         pass_tokens()
         hand_out(3)
     elif chip_i == 0:
         for u in own_units:
-            if u % 8 < OP:
+            if u < OP:
                 pass_unit(u)
         pass_tokens()
         for u in own_units:
-            if u % 8 >= OP:
+            if u >= OP:
                 pass_unit(u)
     else:
-        for u in own_units:
+        tokens_in = _count(_split(topo.mask(home[wi], core), NH)[chip_i - 1])
+        for i, u in enumerate(own_units):
+            if i == HS:
+                g.wait_ge(S.tkh, tokens_in)
+                swap()
             pass_unit(u)
 
-    xo = first if chip_i == 0 else 0
-    x_in = T.xm[:, xo:xo + n]
+    exp = _expected(die, chip_i, core)
+    order = sorted(range(NU), key=lambda u: exp[u])
+
+    def layer1(i, a, b):
+        for j in range(2):
+            t.matmul(T["h%d" % (i % NB)][:, j * m + a:j * m + b], tile(order[i], 0, j), T.x2[:, a:b],
+                     True, True).then_inc(S["l%d" % i], 1)
+
+    def relu(i):
+        s.wait_ge(S["l%d" % i], 4 if i < EARLY else 2)
+        s.activation(T.hb[:, 512 * i:512 * i + 2 * m], T["h%d" % (i % NB)][:, 0:2 * m], Act.Relu).then_inc(S["r%d" % i], 1)
+
+    def layer2(i, q):
+        t.wait_ge(S["r%d" % i], 1)
+        for j in range(2):
+            o = 512 * i + m * j + n * q
+            ins = t.matmul(T["ya%d" % q][:, 0:n], tile(order[i], 1, j), T.hb[:, o:o + n],
+                           i == 0 and j == 0, i == NU - 1 and j == 1)
+            if i == NU - 1 and j == 1:
+                ins.then_inc(S.yd if q == hf else S.yp, 1)
+
     if chip_i == 0:
         t.wait_ge(S.mg2, 1)
     else:
-        ms = _split(topo.mask(home[wi], core), NH)
-        t.wait_ge(S.tkh, _count(ms[chip_i - 1]))
-    exp = _expected(team)[core]
-    order = sorted(range(NU), key=lambda u: exp[u])
-
-    def layer1(i):
-        u = order[i]
-        wait_unit(t, u)
-        for j in range(2):
-            t.matmul(T["h%d" % (i % NB)][:, j * n:(j + 1) * n], T.wb[:, UW * u + 128 * j:UW * u + 128 * (j + 1)],
-                     x_in, True, True).then_inc(S["l%d" % i], 1)
-        s.wait_ge(S["l%d" % i], 2)
-        s.activation(T.hb[:, 256 * i:256 * i + 2 * n], T["h%d" % (i % NB)][:, 0:2 * n], Act.Relu).then_inc(S["r%d" % i], 1)
-
-    def layer2(i):
-        u = order[i]
-        t.wait_ge(S["r%d" % i], 1)
-        for j in range(2):
-            last = i == NU - 1 and j == 1
-            ins = t.matmul(T.yacc[:, 0:n], T.wb[:, UW * u + 256 + 128 * j:UW * u + 384 + 128 * j],
-                           T.hb[:, 256 * i + n * j:256 * i + n * (j + 1)], i == 0 and j == 0, last)
-            if last:
-                ins.then_inc(S.yd, 1)
-
+        t.wait_ge(S.tkh, tokens_in)
+    for i in range(EARLY):
+        wait_unit(t, order[i])
+        layer1(i, n * hf, n * hf + n)
+    t.wait_ge(S.xe, _count(inner))
+    for i in range(EARLY):
+        layer1(i, n * (1 - hf), n * (1 - hf) + n)
+        relu(i)
     for i in range(NU + 2):
-        if i < NU:
-            layer1(i)
-        if i >= 2:
-            layer2(i - 2)
+        if EARLY <= i < NU:
+            wait_unit(t, order[i])
+            layer1(i, 0, m)
+            relu(i)
+        if 2 <= i < NU + 2 - TAIL:
+            layer2(i - 2, 1 - hf)
+            layer2(i - 2, hf)
+    for q in (1 - hf, hf):
+        for i in range(NU - TAIL, NU):
+            layer2(i, q)
 
     slot = RB + 256 * wi + first
     target = T.xw[:, slot:slot + n]
     out = target if side is not None else T.yo[:, 0:n]
+    v.wait_ge(S.yp, 1)
+    v.tensor_copy(T.po[:, 0:n], T["ya%d" % (1 - hf)][:, 0:n]).then_inc(S.pc, 1)
+    g.wait_ge(S.pc, 1)
+    send([(T.po[:, 0:n], T.rp[:, 0:n], [peer], on, S.rp)])
+    v.wait_ge(S.rp, _count(on))
     v.wait_ge(S.yd, 1)
-    v.tensor_copy(out, T.yacc[:, 0:n]).then_inc(S.yc, 1)
+    v.tensor_tensor(out, T["ya%d" % hf][:, 0:n], T.rp[:, 0:n], Op.add).then_inc(S.yc, 1)
     g.wait_ge(S.yc, 1)
     dst = [c for c in ranks if c != core]
     send([(out, target, dst, topo.mask(core, dst[0]), S.res)])
 
     if side is not None:
         total = 0
-        for ci, hv in enumerate(team["chips"]):
+        for hv in team["chips"]:
             for c in hv[0] + hv[1]:
                 if c != core:
                     total += _count(topo.mask(c, core))

import numpy as np
from concourse.bass import DstId, RemoteDMATransfer
from concourse.mybir import dt, AluOpType as Op, AxisListType, ActivationFunctionType as Act

NH = 2
NS = 64
PRE = 2
OP = 4
LG = 2
HS = 1
EARLY = 4
TAIL = 4
NCORES = 96
NU = 8
UW = 512
XB = 4
RB = 2052
NB = 6
WMAX = 8192
CUTS = (0, 256, 640, 1024)

INTS = ("pid", "ri", "g2i", "q7i", "q3i")
COLS = ("m0", "m1", "m2", "g2f", "q7f", "q3f", "w01", "wc", "tcol")
SCRATCH = {
    "cint": ("sbuf", [128, 8], "int32"),
    "cflt": ("sbuf", [128, 16], "float32"),
    "xw": ("sbuf", [128, RB + 2048], "float32"),
    "wb": ("sbuf", [128, NU * UW], "float32"),
    "xg": ("sbuf", [128, 2048], "float32"),
    "ta": ("sbuf", [128, 256], "float32"),
    "tb": ("sbuf", [128, 256], "float32"),
    "xm": ("sbuf", [128, 256], "float32"),
    "x2": ("sbuf", [128, 256], "float32"),
    "hb": ("sbuf", [128, NU * 512], "float32"),
    "po": ("sbuf", [128, 128], "float32"),
    "rp": ("sbuf", [128, 128], "float32"),
    "yo": ("sbuf", [128, 128], "float32"),
    "yb": ("sbuf", [128, 2048], "float32"),
    "win": ("sbuf", [128, WMAX], "bfloat16"),
    "vals": ("sbuf", [128, 256], "bfloat16"),
    "zsel": ("sbuf", [128, 144], "bfloat16"),
    "fa": ("sbuf", [128, 256], "float32"),
    "fb": ("sbuf", [128, 256], "float32"),
    "fc": ("sbuf", [128, 256], "float32"),
    "fd": ("sbuf", [128, 256], "float32"),
    "fsel": ("sbuf", [128, 144], "float32"),
    "fdiff": ("sbuf", [128, 128], "float32"),
    "tri": ("sbuf", [128, 128], "float32"),
    "ki": ("sbuf", [128, 16], "int32"),
    "kf": ("sbuf", [128, 16], "float32"),
    "ones": ("sbuf", [128, 16], "float32"),
    "scn": ("sbuf", [128, 16], "float32"),
    "dump": ("sbuf", [128, 16], "float32"),
    "c16": ("sbuf", [128, 16], "float32"),
    "cz": ("sbuf", [128, 16], "float32"),
    "pa": ("sbuf", [128, 16], "float32"),
    "pb": ("sbuf", [128, 16], "float32"),
    "pp": ("sbuf", [128, 16], "float32"),
    "tq": ("sbuf", [128, 16], "float32"),
    "tqm": ("sbuf", [128, 16], "float32"),
    "ga": ("sbuf", [128, 16], "float32"),
    "gb": ("sbuf", [128, 16], "float32"),
    "gd": ("sbuf", [128, 16], "float32"),
    "ge": ("sbuf", [128, 16], "float32"),
    "offs": ("sbuf", [128, 16], "uint16"),
    "ysrc": ("sbuf", [128, 16], "uint16"),
    "listx": ("sbuf", [128, 64], "uint16"),
    "listy": ("sbuf", [128, 64], "uint16"),
    "ylist": ("sbuf", [128, 128], "uint16"),
    "ydram": ("dram", [128, 16], "uint16"),
    "ya0": ("psum", [128, 512], "float32"),
    "ya1": ("psum", [128, 512], "float32"),
}
for _n in range(NB):
    SCRATCH["h%d" % _n] = ("psum", [128, 512], "float32")

SEMAPHORES = ["io1", "io2", "io3", "io4", "io5", "vs", "sc", "sg", "tm", "tx", "ty", "kq", "kd", "xd", "tka", "tkb",
              "tkh", "xe", "mg1", "mg2", "yp", "yd", "pc", "rp", "yc", "res", "loc", "yl1", "yl2", "fv", "fs", "ys", "yt"]
SEMAPHORES += ["%s%d" % (_k, _n) for _k in ("w", "ld", "l", "r") for _n in range(NU)]


def _count(mask):
    return bin(mask).count("1")


def _split(mask, k):
    eng = [e for e in range(mask.bit_length()) if mask >> e & 1]
    per = 1
    while per * 2 * k <= len(eng):
        per *= 2
    return [sum(1 << e for e in eng[i * per:(i + 1) * per]) for i in range(k)]


def _teams(T, topo):
    homes = []
    for c in T.cores:
        if topo.chip(c) not in homes:
            homes.append(topo.chip(c))
    chips = []
    for c in range(NCORES):
        if topo.chip(c) not in chips:
            chips.append(topo.chip(c))
    teams, used = [], list(homes)
    for h in homes:
        ranks = [c for c in T.cores if topo.chip(c) == h]
        dies = [topo.die(c) for c in ranks]

        def halves(chip):
            out = []
            for s in range(2):
                cs = [c for c in range(NCORES) if topo.chip(c) == chip and topo.die(c) == dies[s]]
                out.append([c for c in cs if c in ranks] + [c for c in cs if c not in ranks])
            return out
        free = [c for c in chips if c not in used and topo.same_plane(h, c)]
        far = [c for c in free if not any(topo.mates(c, x) for x in homes)]
        helpers = (far + [c for c in free if c not in far])[:NH]
        used += helpers
        teams.append({"ranks": ranks, "chips": [halves(h)] + [halves(c) for c in helpers]})
    return teams


def _route(u):
    return [1 + (u + i) % NH for i in range(NH)]


def _reach(u, ci):
    pos = 0 if ci == 0 else 1 + _route(u).index(ci)
    return u // 2 * 2 + (2 if u >= 2 * PRE else 0) + 4.5 * pos


def _order(ci):
    return sorted(range(NU), key=lambda u: (_reach(u, ci), u))


def _owner(die, u, ci):
    return die[1 + u % 3] if ci == 0 else die[u % 4]


def _expected(die, ci, core):
    exp, free = {}, {c: 0.0 for c in die}
    for u in _order(ci):
        own = _owner(die, u, ci)
        a = _reach(u, ci)
        if core == own:
            exp[u] = a
        k = die.index(own)
        t = max(free[own], a + 2)
        for c in die[k + 1:] + die[:k]:
            if ci == 0 and c == die[0]:
                if core == c:
                    exp[u] = u - 10
            else:
                t += 1.1 if ci == 0 else 0.55
                if core == c:
                    exp[u] = t
        free[own] = t
    return exp


def rank_program(g, core, T, topo):
    team = None
    for t in _teams(T, topo):
        for ci, hv in enumerate(t["chips"]):
            if core in hv[0] + hv[1]:
                team, chip_i = t, ci
    if team is None:
        return
    ranks = team["ranks"]
    home = team["chips"][0][0] + team["chips"][0][1]
    mine = team["chips"][chip_i][0] + team["chips"][chip_i][1]
    wi = mine.index(core)
    hf = wi // 4
    die = team["chips"][chip_i][hf]
    peer = mine[(wi + 4) % 8]
    side = ranks.index(core) if core in ranks else None
    n = 256 - NH * NS if chip_i == 0 else NS
    m = 2 * n
    first = NH * NS if chip_i == 0 else (chip_i - 1) * NS
    S = T.sem
    on = topo.mask(core, peer)
    away = topo.mask(core, team["chips"][1 if chip_i == 0 else 0][0][1])
    inner = on & ~away if chip_i == 0 else on
    loc = [0]

    def I(name):
        k = INTS.index(name)
        return T.cint[:, k:k + 1]

    def C(name):
        k = COLS.index(name)
        return T.cflt[:, k:k + 1]

    def did(c):
        rid, pid, _ = topo.addr(c)
        return DstId(rid=rid, pnc=pid)

    def send(parts):
        g.remote_dma_fused([RemoteDMATransfer(dst_ids=[did(c) for c in ds], dma_engine_mask=mk, remote_sem=sem,
                                              srcs=[src], dsts=[dst] * len(ds)) for src, dst, ds, mk, sem in parts],
                           local_sem=S.loc)
        loc[0] += sum(_count(p[3]) for p in parts)

    def unit(u):
        return T.wb[:, UW * u:UW * (u + 1)]

    def tile(u, layer, j):
        c = UW * u + 256 * layer + 128 * j
        return T.wb[:, c:c + 128]

    def part(q):
        return T.x2[:, n * q:n * q + n]

    def wait_unit(q, u):
        if side is not None:
            q.wait_ge(S["ld%d" % u], 32)
            return
        if core != _owner(die, u, chip_i):
            k = _count(inner)
        elif chip_i == 0:
            k = _count(_split(on, 2)[0])
        else:
            r = _route(u)
            p = r.index(chip_i)
            before = r[p - 1] if p else 0
            k = _count(topo.mask(_owner(team["chips"][before][hf], u, before), core))
        q.wait_ge(S["w%d" % u], k)

    def pass_unit(u):
        wait_unit(g, u)
        r = _route(u)
        p = r.index(chip_i) + 1 if chip_i else 0
        if p < len(r):
            nxt = _owner(team["chips"][r[p]][hf], u, r[p])
            send([(unit(u), unit(u), [nxt], topo.mask(core, nxt), S["w%d" % u])])
        k = die.index(core)
        others = [c for c in die[k + 1:] + die[:k] if c not in ranks]
        send([(unit(u), unit(u), others, inner, S["w%d" % u])])

    def swap():
        send([(part(hf), part(hf), [peer], inner, S.xe)])

    def pass_tokens():
        dst = [(team["chips"][k][0] + team["chips"][k][1])[wi] for k in range(1, NH + 1)]
        ms = _split(away, NH)
        g.wait_ge(S.mg1, 1)
        send([(T.xm[:, NS * k:NS * (k + 1)], T.x2[:, NS * hf:NS * hf + NS], [dst[k]], ms[k], S.tkh) for k in range(NH)])
        g.wait_ge(S.mg2, 1)
        swap()

    v, s, t, y = g.vector, g.scalar, g.tensor, g.sync
    nv = [0]

    def did_v(ins):
        ins.then_inc(S.vs, 1)
        nv[0] += 1

    def join():
        v.wait_ge(S.vs, nv[0])

    own_units = [u for u in _order(chip_i) if _owner(die, u, chip_i) == core]

    if side is not None:
        def load(q, u):
            c = 256 * (NU * side + u)
            q.dma_start(T.wb[:, UW * u:UW * u + 256], T.w1[:, c:c + 256]).then_inc(S["ld%d" % u], 16)
            q.dma_start(T.wb[:, UW * u + 256:UW * u + 512], T.w2[:, c:c + 256]).then_inc(S["ld%d" % u], 16)

        y.dma_start(T.ki[:], T.keep[:]).then_inc(S.kd, 16)
        y.sem_inc(S.kq, 1)
        s.wait_ge(S.kq, 1)
        load(y, 0)
        load(s, 1)
        load(y, 2)
        s.dma_start(T.xw[:, XB:RB], T.x[:]).then_inc(S.xd, 16)
        load(y, 3)
        for u in range(4, NU):
            y.wait_ge(S["ld%d" % (u - LG)], 32)
            load(y, u)

        fl = {"allow_small_or_imprecise_dtypes": True}
        g.iota(I("pid"), [[1, 1]], 0, 1).then_inc(S.io1, 1)
        g.iota(T.fdiff[:], [[1, 128]], 0, -1, **fl).then_inc(S.io2, 1)
        g.iota(T.fa[:], [[16, 16], [1, 2], [0, 8]], XB, 0, **fl).then_inc(S.io3, 1)
        g.iota(T.fb[:], [[0, 16], [0, 2], [1, 8]], 0, 0, **fl).then_inc(S.io3, 1)
        g.iota(T.dump[:], [[1, 16]], 4096, 16, **fl).then_inc(S.io4, 1)
        if side == 0:
            g.iota(T.cz[:], [[-1, 16]], -1 - 4096, -16, **fl).then_inc(S.io4, 1)
        else:
            g.iota(T.cz[:], [[-1, 16]], 2048 - 4096, -16, **fl).then_inc(S.io4, 1)
        g.iota(T.fsel[:], [[0, 9], [1, 16]], 0, 0, **fl).then_inc(S.io5, 1)
        g.iota(T.c16[:], [[16, 16]], XB, 0, **fl).then_inc(S.io5, 1)

        did_v(v.memset(T.win[:, 0:2048], 0.0))
        did_v(v.memset(T.xw[:, 0:XB], 0.0))
        did_v(v.memset(T.ones[:], 1.0))
        v.wait_ge(S.io1, 1)
        did_v(v.tensor_scalar(I("ri"), I("pid"), 15, None, Op.bitwise_and))
        did_v(v.tensor_scalar(I("g2i"), I("pid"), 3, 30, Op.logical_shift_right, Op.bitwise_and))
        join()
        did_v(v.tensor_scalar(C("m0"), I("ri"), 0.0, None, Op.is_equal))
        did_v(v.tensor_scalar(C("m1"), I("ri"), 1.0, None, Op.is_equal))
        did_v(v.tensor_scalar(C("m2"), I("ri"), 2.0, None, Op.is_equal))
        did_v(v.tensor_copy(C("g2f"), I("g2i")))
        join()
        s.wait_ge(S.vs, nv[0])
        s.wait_ge(S.io3, 2)
        s.activation(T.fc[:], T.fa[:], Act.Identity, bias=C("m2"), scale=C("m0")).then_inc(S.sc, 1)
        s.activation(T.fd[:], T.fb[:], Act.Identity, scale=C("m1")).then_inc(S.sc, 1)
        v.wait_ge(S.io2, 1)
        did_v(v.tensor_scalar(C("w01"), C("m1"), 256.0, C("m0"), Op.mult, Op.add))
        did_v(v.tensor_scalar(T.tri[:], T.fdiff[:], 0.0, 1.0 if side == 0 else -1.0,
                              Op.is_gt if side == 0 else Op.is_lt, Op.mult))
        v.wait_ge(S.kd, 16)
        did_v(v.tensor_copy(T.kf[:], T.ki[:]))
        join()
        did_v(v.tensor_tensor_scan(T.scn[:], T.ones[:], T.kf[:], 0.0, Op.mult, Op.add))
        did_v(v.tensor_scalar(C("wc"), C("g2f"), C("m2"), C("w01"), Op.mult, Op.add))
        join()
        t.wait_ge(S.vs, nv[0])
        t.matmul(T.h5[:, 0:1], T.tri[:], T.scn[:, 15:16], True, True).then_inc(S.tm, 1)
        v.wait_ge(S.io4, 2)
        did_v(v.tensor_tensor(T.pa[:], T.cz[:], T.scn[:], Op.add if side == 0 else Op.subtract))
        join()
        did_v(v.tensor_tensor(T.pb[:], T.pa[:], T.kf[:], Op.mult))
        join()
        did_v(v.tensor_tensor(T.pp[:], T.pb[:], T.dump[:], Op.add))
        v.wait_ge(S.sc, 2)
        did_v(v.tensor_tensor(T.vals[:], T.fc[:], T.fd[:], Op.add))
        join()
        v.wait_ge(S.tm, 1)
        did_v(v.tensor_scalar(T.offs[:], T.pp[:], T.h5[:, 0:1], None, Op.add))
        join()
        did_v(v.tensor_copy(T.win[:, 0:WMAX].indirect(T.offs[:, 0:16]), T.vals[:]))
        v.wait_ge(S.io5, 2)
        did_v(v.tensor_scalar(T.zsel[:], T.fsel[:], 15.0, C("wc"), Op.is_equal, Op.mult))
        t.wait_ge(S.vs, nv[0])
        for half, bank, sem in ((0, T.h3, S.tx), (1, T.h4, S.ty)):
            for r in range(16):
                ins = t.matmul(bank[:, 0:64], T.zsel[:, 15 - r:143 - r],
                               T.win[:, 1024 * half + r:1024 * half + 1024:16], r == 0, r == 15)
                if r == 15:
                    ins.then_inc(sem, 1)
        after = []
        for half, bank, sem, lst in ((0, T.h3, S.tx, T.listx), (1, T.h4, S.ty, T.listy)):
            v.wait_ge(sem, 1)
            did_v(v.tensor_copy(lst[:], bank[:, 0:64]))
            join()
            s.wait_ge(S.vs, nv[0])
            if half == 0:
                v.wait_ge(S.xd, 16)
                s.wait_ge(S.xd, 16)
            b = 1024 * half
            did_v(v.tensor_copy(T.xg[:, b:b + 512], T.xw[:, 0:RB].indirect(lst[:, 0:32])))
            s.activation(T.xg[:, b + 512:b + 1024], T.xw[:, 0:RB].indirect(lst[:, 32:64]), Act.Copy).then_inc(S.sg, 1)
            after.append(nv[0])

        def hand_out(k):
            ms = _split(on, 2)
            us = [2 * k, 2 * k + 1]
            for u in us:
                g.wait_ge(S["ld%d" % u], 32)
            send([(unit(u), unit(u), [_owner(die, u, 0)], ms[i], S["w%d" % u]) for i, u in enumerate(us)])

        for k in range(PRE):
            hand_out(k)
        land, lsem = (T.ta, S.tka) if side == 0 else (T.tb, S.tkb)
        for half in range(2):
            ms = _split(on, 4)
            g.wait_ge(S.vs, after[half])
            g.wait_ge(S.sg, half + 1)
            send([(T.xg[:, 256 * w:256 * (w + 1)], land[:], [home[w]], ms[w % 4], lsem)
                  for w in range(4 * half, 4 * half + 4) if home[w] != core])

        did_v(v.tensor_scalar(I("q7i"), I("pid"), 7, None, Op.bitwise_and))
        did_v(v.tensor_scalar(I("q3i"), I("pid"), 3, None, Op.logical_shift_right))
        did_v(v.tensor_scalar(T.ga[:], T.pp[:], T.h5[:, 0:1], None, Op.add))
        join()
        did_v(v.tensor_copy(C("q7f"), I("q7i")))
        did_v(v.tensor_copy(C("q3f"), I("q3i")))
        join()
        did_v(v.tensor_scalar(C("tcol"), C("q7f"), 256.0, C("q3f"), Op.mult, Op.add))
        join()
        did_v(v.tensor_scalar(T.tq[:], T.c16[:], C("tcol"), None, Op.add))
        join()
        did_v(v.tensor_scalar(T.tqm[:], T.tq[:], -1.0, float(RB), Op.mult, Op.add))
        join()
        did_v(v.tensor_tensor(T.gb[:], T.ga[:], T.tqm[:], Op.add))
        join()
        did_v(v.tensor_tensor(T.gd[:], T.gb[:], T.kf[:], Op.mult))
        join()
        did_v(v.tensor_tensor(T.ge[:], T.gd[:], T.tq[:], Op.add))
        join()
        did_v(v.tensor_copy(T.ysrc[:], T.ge[:]))
        y.wait_ge(S.vs, nv[0])
        y.dma_start(T.ydram[:], T.ysrc[:]).then_inc(S.yl1, 16)
        y.wait_ge(S.yl1, 16)
        for k in range(8):
            y.dma_start(T.ylist[16 * k:16 * k + 16, :], T.ydram[:]).then_inc(S.yl2, 16)

    if chip_i == 0:
        pa, pb = T.ta, T.tb
        oa = ob = 0
        if side == 0:
            pa, oa = T.xg, 256 * wi
        if side == 1:
            pb, ob = T.xg, 256 * wi
        if side is not None:
            v.wait_ge(S.vs, nv[0])
            v.wait_ge(S.sg, 2)
            t.wait_ge(S.vs, nv[0])
        if side != 0:
            v.wait_ge(S.tka, _count(_split(on, 4)[0]))
        if side != 1:
            v.wait_ge(S.tkb, _count(_split(on, 4)[0]))
        cut = NH * NS
        v.tensor_tensor(T.xm[:, 0:cut], pa[:, oa:oa + cut], pb[:, ob:ob + cut], Op.add).then_inc(S.mg1, 1)
        v.tensor_tensor(part(hf), pa[:, oa + cut:oa + 256], pb[:, ob + cut:ob + 256], Op.add).then_inc(S.mg2, 1)

    tokens_in = 0
    if side is not None:
        hand_out(2)
        pass_tokens()
        hand_out(3)
    elif chip_i == 0:
        for u in own_units:
            if u < OP:
                pass_unit(u)
        pass_tokens()
        for u in own_units:
            if u >= OP:
                pass_unit(u)
    else:
        tokens_in = _count(_split(topo.mask(home[wi], core), NH)[chip_i - 1])
        for i, u in enumerate(own_units):
            if i == HS:
                g.wait_ge(S.tkh, tokens_in)
                swap()
            pass_unit(u)

    exp = _expected(die, chip_i, core)
    order = sorted(range(NU), key=lambda u: exp[u])

    def layer1(i, a, b):
        for j in range(2):
            t.matmul(T["h%d" % (i % NB)][:, j * m + a:j * m + b], tile(order[i], 0, j), T.x2[:, a:b],
                     True, True).then_inc(S["l%d" % i], 1)

    def relu(i):
        s.wait_ge(S["l%d" % i], 4 if i < EARLY else 2)
        s.activation(T.hb[:, 512 * i:512 * i + 2 * m], T["h%d" % (i % NB)][:, 0:2 * m], Act.Relu).then_inc(S["r%d" % i], 1)

    def layer2(i, q):
        t.wait_ge(S["r%d" % i], 1)
        for j in range(2):
            o = 512 * i + m * j + n * q
            ins = t.matmul(T["ya%d" % q][:, 0:n], tile(order[i], 1, j), T.hb[:, o:o + n],
                           i == 0 and j == 0, i == NU - 1 and j == 1)
            if i == NU - 1 and j == 1:
                ins.then_inc(S.yd if q == hf else S.yp, 1)

    if chip_i == 0:
        t.wait_ge(S.mg2, 1)
    else:
        t.wait_ge(S.tkh, tokens_in)
    for i in range(EARLY):
        wait_unit(t, order[i])
        layer1(i, n * hf, n * hf + n)
    t.wait_ge(S.xe, _count(inner))
    for i in range(EARLY):
        layer1(i, n * (1 - hf), n * (1 - hf) + n)
        relu(i)
    for i in range(NU + 2):
        if EARLY <= i < NU:
            wait_unit(t, order[i])
            layer1(i, 0, m)
            relu(i)
        if 2 <= i < NU + 2 - TAIL:
            layer2(i - 2, 1 - hf)
            layer2(i - 2, hf)
    for q in (1 - hf, hf):
        for i in range(NU - TAIL, NU):
            layer2(i, q)

    slot = RB + 256 * wi + first
    target = T.xw[:, slot:slot + n]
    out = target if side is not None else T.yo[:, 0:n]
    v.wait_ge(S.yp, 1)
    v.tensor_copy(T.po[:, 0:n], T["ya%d" % (1 - hf)][:, 0:n]).then_inc(S.pc, 1)
    g.wait_ge(S.pc, 1)
    send([(T.po[:, 0:n], T.rp[:, 0:n], [peer], on, S.rp)])
    v.wait_ge(S.rp, _count(on))
    v.wait_ge(S.yd, 1)
    v.tensor_tensor(out, T["ya%d" % hf][:, 0:n], T.rp[:, 0:n], Op.add).then_inc(S.yc, 1)
    g.wait_ge(S.yc, 1)
    dst = [c for c in ranks if c != core]
    send([(out, target, dst, topo.mask(core, dst[0]), S.res)])

    if side is not None:
        total = 0
        for hv in team["chips"]:
            for c in hv[0] + hv[1]:
                if c != core:
                    total += _count(topo.mask(c, core))
        for q in (v, s):
            q.wait_ge(S.yl2, 128)
            q.wait_ge(S.yc, 1)
            q.wait_ge(S.res, total)
        allx = T.xw[:, 0:RB + 2048]
        for a, b in zip(CUTS, CUTS[1:]):
            for q, o, sem in ((v, 0, S.fv), (s, 1024, S.fs)):
                to, src = T.yb[:, o + a:o + b], allx.indirect(T.ylist[:, (o + a) // 16:(o + b) // 16])
                ins = q.tensor_copy(to, src) if q is v else q.activation(to, src, Act.Copy)
                ins.then_inc(sem, 1)
        for k in range(3):
            a, b = CUTS[k], CUTS[k + 1]
            for q, o, sem, end in ((y, 0, S.fv, S.ys), (s if k == 2 else y, 1024, S.fs, S.yt if k == 2 else S.ys)):
                q.wait_ge(sem, k + 1)
                q.dma_start(T.y[:, o + a:o + b], T.yb[:, o + a:o + b]).then_inc(end, 16)
        y.wait_ge(S.ys, 80)
        s.wait_ge(S.yt, 16)
    g.wait_ge(S.loc, loc[0])
